import numpy as np, ml_dtypes
CORES = [66,74,82,90,194,202,210,218]
N = 8
DEG, TK = 3, 64
MASK = [[0,2,3],[1,4,6],[1,2,5],[1,3,4],[3,4,7],[4,5,7],[5,6,7],[2,3,7]]
def setup_inputs(rng):
    return {"x": rng.standard_normal((N, 128, TK), dtype=np.float32).astype(ml_dtypes.bfloat16), "w": rng.standard_normal((N, 128, DEG * 128), dtype=np.float32).astype(ml_dtypes.bfloat16)}
def setup_inputs_big(rng):
    d = setup_inputs(rng)
    for k in ("x", "w"): d[k] = (d[k].astype(np.float32) * 1024.0).astype(d[k].dtype)
    return d
def setup_inputs_small(rng):
    d = setup_inputs(rng)
    for k in ("x", "w"): d[k] = (d[k].astype(np.float32) * (1 / 1024.0)).astype(d[k].dtype)
    return d
def setup_inputs_apart(rng):
    d = setup_inputs(rng)
    f = (10.0 ** rng.permutation(np.linspace(-1.5, 1.5, N))).astype(np.float32).reshape(N, 1, 1)
    for k in ("x", "w"): d[k] = (d[k].astype(np.float32) * f).astype(d[k].dtype)
    return d
def reference(x, w):
    X, W = x.astype(np.float64), w.astype(np.float64)
    y = np.zeros((N, 128, TK))
    for r in range(N):
        for i, j in enumerate(MASK[r]):
            y[r] += W[r][:, 128 * i:128 * i + 128].T @ X[j]
    return {"y": y.astype(ml_dtypes.bfloat16 if x.dtype != np.float64 else np.float64)}

from concourse.bass import DstId, RemoteDMATransfer

P, TK = 128, 64

SCRATCH = {
    "xin": ("sbuf", [P, 3 * TK], "bfloat16"),
    "ws": ("sbuf", [P, 3 * P], "bfloat16"),
    "acc": ("psum", [P, TK], "float32"),
    "ysb": ("sbuf", [P, TK], "bfloat16"),
}
SEMAPHORES = ["ldx", "ldw", "sent", "mm", "cp", "st"] + ["from%d" % j for j in range(8)]


def _links(topo, a, b):
    return 1 if (topo.mates(a, b) or topo.same_plane(a, b)) else 2


def _dests(T, topo, j):
    mask = T.tables["MASK"]
    ds = [r for r in range(len(mask)) if r != j and j in mask[r]]
    return sorted(ds, key=lambda r: (-_links(topo, T.cores[j], T.cores[r]), r))


def _engines(topo, core, dst_cores):
    m = topo.mask(core, dst_cores[0])
    for d in dst_cores[1:]:
        m &= topo.mask(core, d)
    bits = [e for e in range(16) if (m >> e) & 1]
    n = 1
    while n * 2 <= len(bits):
        n *= 2
    out = 0
    for e in bits[:n]:
        out |= 1 << e
    return out, n


def rank_program(g, core, T, topo):
    rank = T.rank_of(core)
    if rank is None:
        return
    mask = T.tables["MASK"]
    mine = mask[rank]
    own = mine.index(rank)

    def blk(i):
        return T.xin[:, i * TK:(i + 1) * TK]

    g.sync.dma_start(blk(own), T.x[:, :]).then_inc(T.sem.ldx, 16)
    g.sync.dma_start(T.ws[:, :], T.w[:, :]).then_inc(T.sem.ldw, 16)

    ds = _dests(T, topo, rank)
    if ds:
        dcs = [T.cores[r] for r in ds]
        for d in dcs:
            assert topo.may_write(core, d)
        em, ne = _engines(topo, core, dcs)
        ids = []
        for d in dcs:
            rid, pid = topo.addr(d, core)
            ids.append(DstId(rid=rid, pnc=pid))
        outs = [T.xin[:, mask[r].index(rank) * TK:(mask[r].index(rank) + 1) * TK] for r in ds]
        g.wait_ge(T.sem.ldx, 16)
        g.remote_dma_fused(
            [RemoteDMATransfer(dst_ids=ids, dma_engine_mask=em, remote_sem=T.sem["from%d" % rank],
                               srcs=[blk(own)], dsts=outs, alu_op=0)],
            local_sem=T.sem.sent)

    def expected(i):
        j = mine[i]
        return (_dests(T, topo, j).index(rank), _links(topo, T.cores[j], core))

    remote = sorted([i for i in range(len(mine)) if i != own], key=expected)
    g.tensor.wait_ge(T.sem.ldx, 16)
    g.tensor.wait_ge(T.sem.ldw, 16)
    g.tensor.matmul(T.acc[:, :], T.ws[:, own * P:(own + 1) * P], blk(own), start=True, stop=False)
    for k, i in enumerate(remote):
        j = mine[i]
        _, ne_j = _engines(topo, T.cores[j], [T.cores[r] for r in _dests(T, topo, j)])
        g.tensor.wait_ge(T.sem["from%d" % j], ne_j)
        mm = g.tensor.matmul(T.acc[:, :], T.ws[:, i * P:(i + 1) * P], blk(i), start=False, stop=(k == len(remote) - 1))
    mm.then_inc(T.sem.mm, 1)

    g.vector.wait_ge(T.sem.mm, 1)
    g.vector.tensor_copy(T.ysb[:, :], T.acc[:, :]).then_inc(T.sem.cp, 1)
    g.sync.wait_ge(T.sem.cp, 1)
    g.sync.dma_start(T.y[:, :], T.ysb[:, :]).then_inc(T.sem.st, 16)
    g.sync.wait_ge(T.sem.st, 16)
    if ds:
        g.wait_ge(T.sem.sent, ne)
